import numpy as np, ml_dtypes
CORES = [4,20,36,44,92,100,108,116,3,19,35,43,91,99,107,115]
N = 16
TK = 128
COEF = [[2,-1,0,0,0,0,0,0,1,0,0,0,0,0,0,-1],[-1,2,-1,0,0,0,0,0,0,1,0,0,0,0,0,0],[0,-1,2,-1,0,0,0,0,0,0,1,0,0,0,0,0],[0,0,-1,2,-1,0,0,0,0,0,0,1,0,0,0,0],[0,0,0,-1,2,-1,0,0,0,0,0,0,1,0,0,0],[0,0,0,0,-1,2,-1,0,0,0,0,0,0,1,0,0],[0,0,0,0,0,-1,2,-1,0,0,0,0,0,0,1,0],[0,0,0,0,0,0,-1,2,-1,0,0,0,0,0,0,1],[1,0,0,0,0,0,0,-1,2,-1,0,0,0,0,0,0],[0,1,0,0,0,0,0,0,-1,2,-1,0,0,0,0,0],[0,0,1,0,0,0,0,0,0,-1,2,-1,0,0,0,0],[0,0,0,1,0,0,0,0,0,0,-1,2,-1,0,0,0],[0,0,0,0,1,0,0,0,0,0,0,-1,2,-1,0,0],[0,0,0,0,0,1,0,0,0,0,0,0,-1,2,-1,0],[0,0,0,0,0,0,1,0,0,0,0,0,0,-1,2,-1],[-1,0,0,0,0,0,0,1,0,0,0,0,0,0,-1,2]]
def setup_inputs(rng):
    return {"x": rng.standard_normal((N, 128, TK), dtype=np.float32).astype(ml_dtypes.bfloat16), "a": (rng.standard_normal((N, 128, 128), dtype=np.float32) / 11).astype(ml_dtypes.bfloat16)}
def setup_inputs_big(rng):
    d = setup_inputs(rng)
    for k in ("x", "a"): d[k] = (d[k].astype(np.float32) * 1024.0).astype(d[k].dtype)
    return d
def setup_inputs_small(rng):
    d = setup_inputs(rng)
    for k in ("x", "a"): d[k] = (d[k].astype(np.float32) * (1 / 1024.0)).astype(d[k].dtype)
    return d
def setup_inputs_apart(rng):
    d = setup_inputs(rng)
    f = (10.0 ** rng.permutation(np.linspace(-1.5, 1.5, N))).astype(np.float32).reshape(N, 1, 1)
    for k in ("x", "a"): d[k] = (d[k].astype(np.float32) * f).astype(d[k].dtype)
    return d
def reference(x, a):
    X, A = x.astype(np.float64), a.astype(np.float64)
    y = np.stack([A[r].T @ sum(COEF[r][j] * X[j] for j in range(N)) for r in range(N)])
    return {"y": y.astype(ml_dtypes.bfloat16)}

from concourse.bass import DstId, RemoteDMATransfer
from concourse.mybir import AluOpType

BF = "bfloat16"
NIN = 3
NRL = 2
NSC = 2
SCRATCH = {
    "xd": ("dram", [128, 128], BF),
    "xs": ("sbuf", [128, 128], BF),
    "a1": ("sbuf", [128, 128], BF),
    "ps": ("psum", [128, 128], "float32"),
    "ys": ("sbuf", [128, 128], BF),
}
for _i in range(NIN):
    SCRATCH["in%d" % _i] = ("sbuf", [128, 128], BF)
for _i in range(NRL):
    SCRATCH["rl%d" % _i] = ("dram", [128, 128], BF)
for _i in range(NSC):
    SCRATCH["k%d" % _i] = ("sbuf", [128, 128], BF)
    SCRATCH["s%d" % _i] = ("sbuf", [128, 128], BF)
SEMAPHORES = (["xdl", "xsl", "al", "ms", "sc", "sent", "mm", "cp", "st"]
              + ["i%d" % _i for _i in range(NIN)] + ["r%d" % _i for _i in range(NRL)])

FOLD = False
E_COPY = 4
E_ON = 4


def _bits(m):
    return [b for b in range(m.bit_length()) if (m >> b) & 1]


def _mask(bs):
    m = 0
    for b in bs:
        m |= 1 << b
    return m


def _spread(pool, n):
    return pool[::max(1, len(pool) // n)][:n]


def _pow2(n):
    p = 1
    while p * 2 <= n:
        p *= 2
    return p


def _plan(T, topo):
    cores = list(T.cores)
    coef = T.tables["COEF"]
    n = len(cores)

    def on_chip(p, q):
        return topo.chip(cores[p]) == topo.chip(cores[q])

    direct = dict((j, []) for j in range(n))
    groups = []
    for r in range(n):
        far = {}
        for j in range(n):
            c = coef[r][j]
            if j == r or c == 0:
                continue
            if topo.may_write(cores[j], cores[r]):
                direct[j].append(r)
            else:
                far.setdefault(c, []).append(j)
        for c in sorted(far):
            if FOLD:
                groups.append((r, c, far[c]))
            else:
                groups.extend((r, c, [j]) for j in far[c])

    load = dict((q, 0) for q in range(n))
    fwd = dict((q, []) for q in range(n))
    for r, c, js in groups:
        cand = [q for q in range(n) if q != r and q not in js and topo.may_write(cores[q], cores[r])
                and all(topo.may_write(cores[j], cores[q]) for j in js)]
        q = min(cand, key=lambda q: (-sum(on_chip(j, q) for j in js), load[q], q))
        load[q] += 1
        fwd[q].append((r, c, js))
    relays = dict((j, sorted(q for q in range(n) if any(j in js for _, _, js in fwd[q]))) for j in range(n))
    slot, taken = {}, dict((q, set()) for q in range(n))
    for j in sorted(range(n), key=lambda j: (-len(relays[j]), j)):
        if relays[j]:
            s = 0
            while any(s in taken[q] for q in relays[j]):
                s += 1
            slot[j] = s
            for q in relays[j]:
                taken[q].add(s)

    calls = dict((j, []) for j in range(n))
    recv = dict((r, []) for r in range(n))

    def land(r, order, c, count):
        k = len(recv[r])
        recv[r].append((order, c, k, count))
        return k

    for j in range(n):
        me = cores[j]
        dests = set(direct[j]) | set(relays[j]) | set(r for r, _, _ in fwd[j])
        narrow, wide = -1, 0
        for d in dests:
            narrow &= topo.mask(me, cores[d])
            wide |= topo.mask(me, cores[d])
        narrow, wide = _bits(narrow), _bits(wide)
        used = []
        if relays[j]:
            eng = _spread(narrow, E_COPY)
            used += eng
            calls[j].append(([], [(eng, "r%d" % slot[j], ["xd"], [(q, "rl%d" % slot[j]) for q in relays[j]])]))
        offw = [r for r in direct[j] if not on_chip(j, r)]
        onw = [r for r in direct[j] if on_chip(j, r)]
        xf, busy = [], []
        if offw:
            pool = used if used else narrow
            share = _pow2(len(pool) // len(offw))
            for i, r in enumerate(offw):
                eng = pool[i * share:(i + 1) * share]
                busy += eng
                k = land(r, 1, coef[r][j], len(eng))
                xf.append((eng, "i%d" % k, ["xd"], [(r, "in%d" % k)]))
        for r in onw:
            free = [b for b in wide if b not in busy]
            old = [b for b in free if b in used]
            new = [b for b in free if b not in narrow] or free
            eng = _spread(old, E_ON) if len(old) >= E_ON else _spread(new, E_ON)
            busy += eng
            k = land(r, 0, coef[r][j], len(eng))
            xf.append((eng, "i%d" % k, ["xd"], [(r, "in%d" % k)]))
        if xf:
            calls[j].append(([], xf))
        sets = []
        for _, _, js in fwd[j]:
            if js not in sets:
                sets.append(js)
        sets.sort(key=lambda js: sum(not on_chip(i, j) for i in js))
        for js in sets:
            terms = [t for t in fwd[j] if t[2] == js]
            share = _pow2(len(narrow) // len(terms))
            xf = []
            for i, (r, c, _) in enumerate(terms):
                eng = narrow[i * share:(i + 1) * share]
                k = land(r, 2, c, len(eng))
                xf.append((eng, "i%d" % k, ["rl%d" % slot[s] for s in js], [(r, "in%d" % k)]))
            calls[j].append(([("r%d" % slot[s], E_COPY) for s in js], xf))
    return calls, recv


def rank_program(g, core, T, topo):
    rank = T.rank_of(core)
    if rank is None:
        return
    cores = list(T.cores)
    coef = T.tables["COEF"]
    calls, recv = _plan(T, topo)
    sem = T.sem

    g.sync.dma_start(T.xd[:], T.x[:]).then_inc(sem.xdl, 16)
    g.sync.dma_start(T.xs[:], T.x[:]).then_inc(sem.xsl, 16)
    g.sync.dma_start(T.a1[:], T.a[:]).then_inc(sem.al, 16)

    terms = sorted(recv[rank], key=lambda t: (t[0], -t[3]))
    cs = []
    for c in [coef[rank][rank]] + [t[1] for t in terms]:
        if c != 1 and c not in cs:
            cs.append(c)
    for i, c in enumerate(cs):
        g.vector.memset(T["k%d" % i][:], float(c)).then_inc(sem.ms, 1)
    if cs:
        g.vector.wait_ge(sem.ms, len(cs))
        g.vector.wait_ge(sem.al, 16)
    for i, c in enumerate(cs):
        g.vector.tensor_tensor(T["s%d" % i][:], T.a1[:], T["k%d" % i][:], AluOpType.mult).then_inc(sem.sc, 1)

    def lhs(c):
        return T.a1[:] if c == 1 else T["s%d" % cs.index(c)][:]

    g.wait_ge(sem.xdl, 16)
    left = 0
    for waits, xfers in calls[rank]:
        for s, v in waits:
            g.wait_ge(sem[s], v)
        ts = []
        for eng, s, srcs, dsts in xfers:
            ids = []
            for d, _ in dsts:
                rid, pid, _se = topo.addr(cores[d])
                ids.append(DstId(rid=rid, pnc=pid))
            ts.append(RemoteDMATransfer(dst_ids=ids, dma_engine_mask=_mask(eng), remote_sem=sem[s],
                                        srcs=[T[b][:] for b in srcs], dsts=[T[b][:] for _, b in dsts],
                                        alu_op=1 if len(srcs) > 1 else 0))
            left += len(eng)
        g.remote_dma_fused(ts, local_sem=sem.sent)

    g.tensor.wait_ge(sem.al, 16)
    if cs:
        g.tensor.wait_ge(sem.sc, len(cs))
    g.tensor.wait_ge(sem.xsl, 16)
    mm = g.tensor.matmul(T.ps[:], lhs(coef[rank][rank]), T.xs[:], True, not terms)
    for i, (_, c, k, count) in enumerate(terms):
        g.tensor.wait_ge(sem["i%d" % k], count)
        mm = g.tensor.matmul(T.ps[:], lhs(c), T["in%d" % k][:], False, i == len(terms) - 1)
    mm.then_inc(sem.mm, 1)

    g.vector.wait_ge(sem.mm, 1)
    g.vector.tensor_copy(T.ys[:], T.ps[:]).then_inc(sem.cp, 1)
    g.sync.wait_ge(sem.cp, 1)
    g.sync.dma_start(T.y[:], T.ys[:]).then_inc(sem.st, 16)
    g.sync.wait_ge(sem.st, 16)
    if left:
        g.wait_ge(sem.sent, left)
